import numpy as np
import ml_dtypes


def mxq(x, axis, fmt="e4m3"):
    dtype, down = {"e4m3": (ml_dtypes.float8_e4m3fn, 7), "e5m2": (ml_dtypes.float8_e5m2, 14)}[fmt]
    v = np.moveaxis(np.asarray(x, np.float32).astype(ml_dtypes.bfloat16).astype(np.float64), axis, -1)
    blocks = v.reshape(v.shape[:-1] + (-1, 32))
    amax = np.abs(blocks).max(-1, keepdims=True)
    byte = np.maximum(np.where(amax > 0, np.frexp(amax)[1] - 1 + 127, 0) - down, 1)
    scale = np.exp2(byte - 127.0)
    codes = (blocks / scale).astype(np.float32).astype(dtype).astype(np.float64)
    return np.moveaxis((codes * scale).reshape(v.shape), -1, axis)


WIDE = False


def mx_kscale(k):
    if not WIDE:
        return np.ones(k)
    levels = np.array([30, -30])
    if k % 512:
        return np.exp2(np.random.permutation(np.resize(levels, k // 32))).repeat(32)
    a = np.empty((k // 512, 16))
    for p in range(k // 512):
        a[p, :8] = np.random.permutation(np.resize(levels, 8))
        for g in range(8):
            far = levels[np.abs(levels - a[p, g]) >= 10]
            a[p, g + 8] = far[np.random.randint(len(far))]
    return np.exp2(a.ravel()).repeat(32)


def f64(x):
    return np.asarray(x).astype(np.float64)


def striped(idx):
    return np.tile(np.asarray(idx).reshape(-1, 16).T, (8, 1)).astype(np.uint16)


def unstriped(offs):
    return offs[:16].T.reshape(-1).astype(np.int64)


E2M1 = np.array([0.0, 0.5, 1.0, 1.5, 2.0, 3.0, 4.0, 6.0, -0.0, -0.5, -1.0, -1.5, -2.0, -3.0, -4.0, -6.0])


def pack_weight(w, fmt):
    k, n = w.shape
    w = f64(np.asarray(w, np.float32).astype(ml_dtypes.bfloat16)).reshape(k // 32, 32, n)
    amax = np.abs(w).max(1)
    if fmt in ("e4m3", "e5m2"):
        byte = np.frexp(amax)[1] - 1 + 127 - (7 if fmt == "e4m3" else 14)
    else:
        mant, ex = np.frexp(amax / 6.0)
        byte = np.where(mant > 0.5, ex, ex - 1) + 127
    byte = np.clip(np.where(amax > 0, byte, 1), 1, 254)
    scaled = (w * np.exp2(127.0 - byte)[:, None, :]).reshape(k, n).astype(np.float32)
    by_word = np.ascontiguousarray(scaled.reshape(k // 512, 128, 4, n).transpose(0, 1, 3, 2))
    if fmt in ("e4m3", "e5m2"):
        words = by_word.astype(ml_dtypes.float8_e4m3fn if fmt == "e4m3" else ml_dtypes.float8_e5m2).view(np.uint8)
    else:
        c = by_word.astype(ml_dtypes.float4_e2m1fn).view(np.uint8) & 0xF
        words = (c[..., 0::2] | (c[..., 1::2] << 4)).reshape(k // 512, 128, 2 * n)
    return np.ascontiguousarray(words), np.ascontiguousarray(byte.astype(np.uint8).reshape(k // 512, 16, n))


def unpack_weight(words, scales, fmt):
    g, _, n = scales.shape
    words = np.ascontiguousarray(words).reshape(g, 128, n, -1)
    if fmt in ("e4m3", "e5m2"):
        vals = words.view(ml_dtypes.float8_e4m3fn if fmt == "e4m3" else ml_dtypes.float8_e5m2).astype(np.float64)
    else:
        nib = np.empty((g, 128, n, 4), np.uint8)
        nib[..., 0::2] = words & 0xF
        nib[..., 1::2] = words >> 4
        vals = E2M1[nib]
    vals = vals * np.repeat(np.exp2(scales.astype(np.float64) - 127.0), 8, axis=1)[..., None]
    return vals.transpose(0, 1, 3, 2).reshape(g * 512, n)


def sigmoid(v):
    return 1.0 / (1.0 + np.exp(-v))


K, T, Z, J, R, Q, N, S, E = 512, 1024, 1024, 256, 512, 1024, 256, 1024, 1024


def setup_inputs():
    n = np.random.standard_normal
    idx = np.random.permutation(T)[:J]
    idx2 = np.random.permutation(Z)[:J]
    idx3 = np.random.permutation(J)[:J]
    idx4 = np.random.permutation(Q)[:J]
    idx5 = np.random.permutation(S)[:N]
    idx6 = np.random.permutation(E)[:J]
    fk = mx_kscale(K)
    fr = mx_kscale(R)
    xtp = pack_weight(n((K, T)) / fk[:, None], "e5m2")
    xop = pack_weight(n((K, Z)) / fk[:, None], "e4m3")
    wp = pack_weight(n((K, R)) * 1 / np.sqrt(K) * fk[:, None] * fr, "e2m1")
    vsp = pack_weight(n((R, S)) * 1 / np.sqrt(R) / fr[:, None], "e2m1")
    return {
        "xt_words": xtp[0],
        "xt_scales": xtp[1],
        "xo_words": xop[0],
        "xo_scales": xop[1],
        "w_words": wp[0],
        "w_scales": wp[1],
        "tg": (1.0 * n((R, Q))).astype(np.float32),
        "sg": (np.random.uniform(0.6, 1.6, (R, 1))).astype(np.float32),
        "bg": (np.random.uniform(-1.0, 1.0, (R, 1))).astype(np.float32),
        "vs_words": vsp[0],
        "vs_scales": vsp[1],
        "offs": striped(idx),
        "offs2": striped(idx2),
        "offs3": striped(idx3),
        "offs4": striped(idx4),
        "offs5": striped(idx5),
        "offs6": striped(idx6),
    }


def reference(xt_words, xt_scales, xo_words, xo_scales, w_words, w_scales, tg, sg, bg, vs_words, vs_scales, offs, offs2, offs3, offs4, offs5, offs6):
    idx = unstriped(offs)
    idx2 = unstriped(offs2)
    idx3 = unstriped(offs3)
    idx4 = unstriped(offs4)
    idx5 = unstriped(offs5)
    idx6 = unstriped(offs6)
    xtu = unpack_weight(xt_words, xt_scales, "e5m2")
    xou = unpack_weight(xo_words, xo_scales, "e4m3")
    wu = unpack_weight(w_words, w_scales, "e2m1")
    vsu = unpack_weight(vs_words, vs_scales, "e2m1")
    xtidxg = xtu[:, idx]
    a = wu.T @ xtidxg
    xoidx2g = xou[:, idx2]
    b = wu.T @ xoidx2g
    hid = np.abs(a - b[:, idx3]) * sigmoid(f64(tg)[:, idx4] * f64(sg) + f64(bg))
    vsidx5g = vsu[:, idx5]
    hidq = mxq(hid, 0, "e4m3")
    p = vsidx5g.T @ hidq
    y = np.zeros((N, E))
    y[:, idx6] = p
    return y

@@ -1,0 +1,163 @@
+from contextlib import ExitStack
+
+import concourse.mybir as mybir
+
+K, T, J, R, N, E = 512, 1024, 256, 512, 256, 1024
+FLOPS = 2 * (2 * K * R * J + R * N * J)
+
+F32 = mybir.dt.float32
+BF16 = mybir.dt.bfloat16
+I32 = mybir.dt.int32
+U32 = mybir.dt.uint32
+U16 = mybir.dt.uint16
+U8 = mybir.dt.uint8
+E4M3 = mybir.dt.float8_e4m3fn_x4
+E5M2 = mybir.dt.float8_e5m2_x4
+E2M1 = mybir.dt.float4_e2m1fn_x4
+ACT = mybir.ActivationFunctionType
+ALU = mybir.AluOpType
+
+P = 128
+PACK = 4
+HALF = J // 2
+
+
+def tile_list_tablepartner_oneforboth_store_scattered_kernel(
+    tc, xt_words, xt_scales, xo_words, xo_scales, w_words, w_scales, tg, sg, bg, vs_words, vs_scales,
+    offs, offs2, offs3, offs4, offs5, offs6, out,
+):
+    nc = tc.nc
+    with ExitStack() as ctx:
+        lists = ctx.enter_context(tc.tile_pool(name="lists", bufs=1))
+        keep = ctx.enter_context(tc.tile_pool(name="keep", bufs=1))
+        psum = ctx.enter_context(tc.psum_pool(name="psum", bufs=1))
+
+        def load_list(src, name):
+            tile = lists.tile([P, J // 16], U16, name=name)
+            nc.sync.dma_start(tile[:], src)
+            return tile
+
+        def scale_tile(engine, width, name):
+            tile = keep.tile([P, width], U8, name=name, align_bytes=64)
+            engine.memset(tile[:].bitcast(I32), 0)
+            return tile
+
+        def load_scales(queue, tile, src, quadrants):
+            for q in quadrants:
+                queue.dma_start(tile[32 * q : 32 * q + 4, :].bitcast(I32), src[0, 4 * q : 4 * q + 4, :].bitcast(I32))
+
+        xo_sc = scale_tile(nc.gpsimd, T, "xo_sc")
+        w_sc = scale_tile(nc.gpsimd, R, "w_sc")
+        xt_sc = scale_tile(nc.vector, T, "xt_sc")
+        vs_sc = scale_tile(nc.vector, T, "vs_sc")
+
+        w_raw = keep.tile([P, R], U16, name="w_raw", align_bytes=64)
+        xo_w = keep.tile([P, T], U32, name="xo_w", align_bytes=64)
+        xt_w = keep.tile([P, T], U32, name="xt_w", align_bytes=64)
+        vs_w = keep.tile([P, T], U16, name="vs_w", align_bytes=64)
+        tg_rows = [keep.tile([P, T], F32, name=f"tg{t}") for t in range(PACK)]
+        tg_view = tg.rearrange("(p t) q -> p t q", t=PACK)
+        slope = keep.tile([P, PACK], F32, name="slope")
+        shift = keep.tile([P, PACK], F32, name="shift")
+
+        l_xo = load_list(offs2, "l_xo")
+        nc.sync.dma_start(w_raw[:].bitcast(I32), w_words[0].bitcast(I32))
+        nc.sync.dma_start(xo_w[:].bitcast(I32), xo_words[0].rearrange("p c t -> p (c t)").bitcast(I32))
+        nc.sync.dma_start(xt_w[:].bitcast(I32), xt_words[0].rearrange("p c t -> p (c t)").bitcast(I32))
+        l_xt = load_list(offs, "l_xt")
+        l_b = load_list(offs3, "l_b")
+        nc.sync.dma_start(tg_rows[0][:], tg_view[:, 0, :])
+        l_tg = load_list(offs4, "l_tg")
+        nc.sync.dma_start(slope[:], sg.rearrange("(p t) o -> p (t o)", t=PACK))
+        nc.sync.dma_start(shift[:], bg.rearrange("(p t) o -> p (t o)", t=PACK))
+        nc.sync.dma_start(tg_rows[1][:], tg_view[:, 1, :])
+        nc.sync.dma_start(vs_w[:].bitcast(I32), vs_words[0].bitcast(I32))
+        l_vs = load_list(offs5, "l_vs")
+        nc.sync.dma_start(tg_rows[2][:], tg_view[:, 2, :])
+        nc.sync.dma_start(tg_rows[3][:], tg_view[:, 3, :])
+        l_out = load_list(offs6, "l_out")
+
+        load_scales(nc.scalar, xo_sc, xo_scales, range(4))
+        load_scales(nc.gpsimd, w_sc, w_scales, range(2))
+        load_scales(nc.scalar, w_sc, w_scales, range(2, 4))
+        load_scales(nc.gpsimd, xt_sc, xt_scales, range(2))
+        load_scales(nc.scalar, xt_sc, xt_scales, range(2, 4))
+        load_scales(nc.gpsimd, vs_sc, vs_scales, range(4))
+        pages = [keep.tile([P, E], F32, name=f"page{n}") for n in range(N // P)]
+        for page in pages:
+            nc.vector.memset(page[:], 0.0)
+
+        w_cols = keep.tile([P, PACK, P], U16, name="w_cols", align_bytes=64)
+        w_col_sc = keep.tile([P, PACK, P], U8, name="w_col_sc", align_bytes=64)
+        nc.vector.tensor_copy(w_cols[:], w_raw[:].rearrange("p (m t) -> p t m", t=PACK))
+        nc.vector.tensor_copy(w_col_sc[:], w_sc[:].rearrange("p (m t) -> p t m", t=PACK))
+
+        def gather(words, scales, offsets, name):
+            got = keep.tile([P, J], words.dtype, name=name + "_w", align_bytes=64)
+            got_sc = keep.tile([P, J], U8, name=name + "_sc", align_bytes=64)
+            nc.vector.tensor_copy(got[:], words[:].indirect(offsets[:]))
+            nc.vector.tensor_copy(got_sc[:], scales[:].indirect(offsets[:]))
+            return got, got_sc
+
+        xo_g, xo_g_sc = gather(xo_w, xo_sc, l_xo, "xo_g")
+        b_ps = [psum.tile([P, J], F32, name=f"b_ps{t}", tag=f"bank{t}") for t in range(PACK)]
+        for t in range(PACK):
+            nc.tensor.matmul_mx(b_ps[t][:], lhsT=w_cols[:, t, :].bitcast(E2M1), lhsT_scale=w_col_sc[:, t, :],
+                                rhs=xo_g[:].bitcast(E4M3), rhs_scale=xo_g_sc[:], start=True, stop=True)
+        xt_g, xt_g_sc = gather(xt_w, xt_sc, l_xt, "xt_g")
+        a_ps = [psum.tile([P, 2, J], F32, name=f"a_ps{u}") for u in range(2)]
+        for t in range(PACK):
+            nc.tensor.matmul_mx(a_ps[t // 2][:, t % 2, :], lhsT=w_cols[:, t, :].bitcast(E2M1), lhsT_scale=w_col_sc[:, t, :],
+                                rhs=xt_g[:].bitcast(E5M2), rhs_scale=xt_g_sc[:], start=True, stop=True)
+
+        b_sb = [keep.tile([P, 2 * J], F32, name=f"b_sb{t}") for t in range(PACK)]
+        for t in range(PACK):
+            nc.scalar.copy(b_sb[t][:, 0:J], b_ps[t][:])
+        partner = [keep.tile([P, 2, J], F32, name=f"partner{u}") for u in range(2)]
+        for t in range(PACK):
+            if t < 2:
+                nc.vector.tensor_copy(partner[0][:, t, :], b_sb[t][:].indirect(l_b[:]))
+            else:
+                nc.scalar.activation(partner[1][:, t - 2, :], b_sb[t][:].indirect(l_b[:]), ACT.Copy)
+        diff = [keep.tile([P, 2, J], F32, name=f"diff{u}") for u in range(2)]
+        size = keep.tile([P, PACK, J], F32, name="size")
+        for u in range(2):
+            nc.vector.tensor_tensor(diff[u][:], a_ps[u][:], partner[u][:], ALU.subtract)
+            nc.scalar.activation(size[:, 2 * u : 2 * u + 2, :], diff[u][:], ACT.Abs)
+
+        gate = keep.tile([P, PACK, J], F32, name="gate")
+        for t in range(PACK):
+            nc.scalar.activation(gate[:, t, :], tg_rows[t][:].indirect(l_tg[:]), ACT.Sigmoid,
+                                 bias=shift[:, t : t + 1], scale=slope[:, t : t + 1])
+
+        vs_g, vs_g_sc = gather(vs_w, vs_sc, l_vs, "vs_g")
+
+        hid = [keep.tile([P, HALF * PACK], BF16, name=f"hid{h}", align_bytes=64) for h in range(2)]
+        hid_q = [keep.tile([P, HALF], U32, name=f"hid_q{h}", align_bytes=64) for h in range(2)]
+        hid_sc = [keep.tile([P, HALF], U8, name=f"hid_sc{h}", align_bytes=64) for h in range(2)]
+        for h in range(2):
+            cols = slice(h * HALF, (h + 1) * HALF)
+            nc.vector.tensor_tensor(
+                hid[h][:].rearrange("p (c i t) -> p c t i", i=4, t=PACK),
+                size[:, :, cols].rearrange("p t (c i) -> p c t i", i=4),
+                gate[:, :, cols].rearrange("p t (c i) -> p c t i", i=4),
+                ALU.mult,
+            )
+        for h in range(2):
+            nc.vector.quantize_mx(hid_q[h][:].bitcast(E4M3), hid_sc[h][:], hid[h][:])
+        for h in range(2):
+            places = l_out[:, h * HALF // 16 : (h + 1) * HALF // 16]
+            for n in range(N // P):
+                rows = slice(n * P, (n + 1) * P)
+                p_ps = psum.tile([P, HALF], F32, name=f"p_ps{h}{n}", tag=f"bank{2 * h + n}")
+                nc.tensor.matmul_mx(p_ps[:], lhsT=vs_g[:, rows].bitcast(E2M1), lhsT_scale=vs_g_sc[:, rows],
+                                    rhs=hid_q[h][:].bitcast(E4M3), rhs_scale=hid_sc[h][:], start=True, stop=True)
+                p_sb = keep.tile([P, HALF], F32, name=f"p_sb{h}{n}")
+                if n == 0:
+                    nc.vector.tensor_copy(p_sb[:], p_ps[:])
+                    nc.vector.tensor_copy(pages[n][:].indirect(places), p_sb[:])
+                else:
+                    nc.scalar.copy(p_sb[:], p_ps[:])
+                    nc.scalar.activation(pages[n][:].indirect(places), p_sb[:], ACT.Copy)
+        nc.sync.dma_start(out[0:P, :], pages[0][:])
+        nc.scalar.dma_start(out[P : 2 * P, :], pages[1][:])

@@ -46,9 +46,9 @@ def tile_list_tablepartner_oneforboth_store_scattered_kernel(
             for q in quadrants:
                 queue.dma_start(tile[32 * q : 32 * q + 4, :].bitcast(I32), src[0, 4 * q : 4 * q + 4, :].bitcast(I32))
 
-        xo_sc = scale_tile(nc.gpsimd, T, "xo_sc")
-        w_sc = scale_tile(nc.gpsimd, R, "w_sc")
+        xo_sc = scale_tile(nc.vector, T, "xo_sc")
         xt_sc = scale_tile(nc.vector, T, "xt_sc")
+        w_sc = scale_tile(nc.vector, R, "w_sc")
         vs_sc = scale_tile(nc.vector, T, "vs_sc")
 
         w_raw = keep.tile([P, R], U16, name="w_raw", align_bytes=64)
@@ -60,29 +60,42 @@ def tile_list_tablepartner_oneforboth_store_scattered_kernel(
         slope = keep.tile([P, PACK], F32, name="slope")
         shift = keep.tile([P, PACK], F32, name="shift")
 
-        l_xo = load_list(offs2, "l_xo")
         nc.sync.dma_start(w_raw[:].bitcast(I32), w_words[0].bitcast(I32))
+        l_xo = load_list(offs2, "l_xo")
+        load_scales(nc.sync, xo_sc, xo_scales, [0])
+        load_scales(nc.sync, xo_sc, xo_scales, [1])
+        load_scales(nc.sync, xo_sc, xo_scales, [2])
+        load_scales(nc.sync, xo_sc, xo_scales, [3])
+        load_scales(nc.sync, w_sc, w_scales, [0])
         nc.sync.dma_start(xo_w[:].bitcast(I32), xo_words[0].rearrange("p c t -> p (c t)").bitcast(I32))
-        nc.sync.dma_start(xt_w[:].bitcast(I32), xt_words[0].rearrange("p c t -> p (c t)").bitcast(I32))
+        load_scales(nc.sync, w_sc, w_scales, [1])
+        load_scales(nc.sync, w_sc, w_scales, [2])
+        load_scales(nc.sync, w_sc, w_scales, [3])
         l_xt = load_list(offs, "l_xt")
-        l_b = load_list(offs3, "l_b")
+        nc.sync.dma_start(xt_w[:].bitcast(I32), xt_words[0].rearrange("p c t -> p (c t)").bitcast(I32))
+        load_scales(nc.sync, xt_sc, xt_scales, [0])
+        load_scales(nc.sync, xt_sc, xt_scales, [1])
         nc.sync.dma_start(tg_rows[0][:], tg_view[:, 0, :])
+        l_b = load_list(offs3, "l_b")
         l_tg = load_list(offs4, "l_tg")
         nc.sync.dma_start(slope[:], sg.rearrange("(p t) o -> p (t o)", t=PACK))
-        nc.sync.dma_start(shift[:], bg.rearrange("(p t) o -> p (t o)", t=PACK))
         nc.sync.dma_start(tg_rows[1][:], tg_view[:, 1, :])
-        nc.sync.dma_start(vs_w[:].bitcast(I32), vs_words[0].bitcast(I32))
-        l_vs = load_list(offs5, "l_vs")
+        nc.sync.dma_start(shift[:], bg.rearrange("(p t) o -> p (t o)", t=PACK))
         nc.sync.dma_start(tg_rows[2][:], tg_view[:, 2, :])
+        l_vs = load_list(offs5, "l_vs")
+        load_scales(nc.sync, vs_sc, vs_scales, [0])
+        load_scales(nc.sync, vs_sc, vs_scales, [1])
         nc.sync.dma_start(tg_rows[3][:], tg_view[:, 3, :])
         l_out = load_list(offs6, "l_out")
+        nc.sync.dma_start(vs_w[:].bitcast(I32), vs_words[0].bitcast(I32))
+        load_scales(nc.gpsimd, xt_sc, xt_scales, [2])
+        load_scales(nc.gpsimd, xt_sc, xt_scales, [3])
+        load_scales(nc.gpsimd, vs_sc, vs_scales, [2])
+        load_scales(nc.gpsimd, vs_sc, vs_scales, [3])
 
-        load_scales(nc.scalar, xo_sc, xo_scales, range(4))
-        load_scales(nc.gpsimd, w_sc, w_scales, range(2))
-        load_scales(nc.scalar, w_sc, w_scales, range(2, 4))
-        load_scales(nc.gpsimd, xt_sc, xt_scales, range(2))
-        load_scales(nc.scalar, xt_sc, xt_scales, range(2, 4))
-        load_scales(nc.gpsimd, vs_sc, vs_scales, range(4))
+        warm = keep.tile([P, 2], F32, name="warm")
+        nc.vector.memset(warm[:, 0:1], 0.0)
+        nc.scalar.activation(warm[:, 1:2], warm[:, 0:1], ACT.Sigmoid)
         pages = [keep.tile([P, E], F32, name=f"page{n}") for n in range(N // P)]
         for page in pages:
             nc.vector.memset(page[:], 0.0)
@@ -90,7 +103,9 @@ def tile_list_tablepartner_oneforboth_store_scattered_kernel(
         w_cols = keep.tile([P, PACK, P], U16, name="w_cols", align_bytes=64)
         w_col_sc = keep.tile([P, PACK, P], U8, name="w_col_sc", align_bytes=64)
         nc.vector.tensor_copy(w_cols[:], w_raw[:].rearrange("p (m t) -> p t m", t=PACK))
-        nc.vector.tensor_copy(w_col_sc[:], w_sc[:].rearrange("p (m t) -> p t m", t=PACK))
+        w_sc_view = w_sc[:].rearrange("p (m t) -> p t m", t=PACK)
+        nc.vector.tensor_copy(w_col_sc[:, 0, :], w_sc_view[:, 0, :])
+        nc.vector.tensor_copy(w_col_sc[:, 1:PACK, :], w_sc_view[:, 1:PACK, :])
 
         def gather(words, scales, offsets, name):
             got = keep.tile([P, J], words.dtype, name=name + "_w", align_bytes=64)
@@ -115,20 +130,22 @@ def tile_list_tablepartner_oneforboth_store_scattered_kernel(
             nc.scalar.copy(b_sb[t][:, 0:J], b_ps[t][:])
         partner = [keep.tile([P, 2, J], F32, name=f"partner{u}") for u in range(2)]
         for t in range(PACK):
+            picked = partner[t // 2][:, t % 2, :]
             if t < 2:
-                nc.vector.tensor_copy(partner[0][:, t, :], b_sb[t][:].indirect(l_b[:]))
+                nc.vector.tensor_copy(picked, b_sb[t][:].indirect(l_b[:]))
             else:
-                nc.scalar.activation(partner[1][:, t - 2, :], b_sb[t][:].indirect(l_b[:]), ACT.Copy)
-        diff = [keep.tile([P, 2, J], F32, name=f"diff{u}") for u in range(2)]
-        size = keep.tile([P, PACK, J], F32, name="size")
+                nc.scalar.activation(picked, b_sb[t][:].indirect(l_b[:]), ACT.Copy)
+        diff = keep.tile([P, PACK, J], F32, name="diff")
         for u in range(2):
-            nc.vector.tensor_tensor(diff[u][:], a_ps[u][:], partner[u][:], ALU.subtract)
-            nc.scalar.activation(size[:, 2 * u : 2 * u + 2, :], diff[u][:], ACT.Abs)
+            nc.vector.tensor_tensor(diff[:, 2 * u : 2 * u + 2, :], a_ps[u][:], partner[u][:], ALU.subtract)
 
         gate = keep.tile([P, PACK, J], F32, name="gate")
         for t in range(PACK):
             nc.scalar.activation(gate[:, t, :], tg_rows[t][:].indirect(l_tg[:]), ACT.Sigmoid,
                                  bias=shift[:, t : t + 1], scale=slope[:, t : t + 1])
+
+        gated = keep.tile([P, PACK, J], F32, name="gated")
+        nc.vector.tensor_tensor(gated[:, 0:2, :], diff[:, 0:2, :], gate[:, 0:2, :], ALU.mult)
 
         vs_g, vs_g_sc = gather(vs_w, vs_sc, l_vs, "vs_g")
 
@@ -137,11 +154,11 @@ def tile_list_tablepartner_oneforboth_store_scattered_kernel(
         hid_sc = [keep.tile([P, HALF], U8, name=f"hid_sc{h}", align_bytes=64) for h in range(2)]
         for h in range(2):
             cols = slice(h * HALF, (h + 1) * HALF)
-            nc.vector.tensor_tensor(
+            nc.vector.tensor_tensor(gated[:, 2:4, cols], diff[:, 2:4, cols], gate[:, 2:4, cols], ALU.mult)
+            nc.scalar.activation(
                 hid[h][:].rearrange("p (c i t) -> p c t i", i=4, t=PACK),
-                size[:, :, cols].rearrange("p t (c i) -> p c t i", i=4),
-                gate[:, :, cols].rearrange("p t (c i) -> p c t i", i=4),
-                ALU.mult,
+                gated[:, :, cols].rearrange("p t (c i) -> p c t i", i=4),
+                ACT.Abs,
             )
         for h in range(2):
             nc.vector.quantize_mx(hid_q[h][:].bitcast(E4M3), hid_sc[h][:], hid[h][:])
@@ -154,10 +171,10 @@ def tile_list_tablepartner_oneforboth_store_scattered_kernel(
                                     rhs=hid_q[h][:].bitcast(E4M3), rhs_scale=hid_sc[h][:], start=True, stop=True)
                 p_sb = keep.tile([P, HALF], F32, name=f"p_sb{h}{n}")
                 if n == 0:
-                    nc.vector.tensor_copy(p_sb[:], p_ps[:])
-                    nc.vector.tensor_copy(pages[n][:].indirect(places), p_sb[:])
-                else:
                     nc.scalar.copy(p_sb[:], p_ps[:])
                     nc.scalar.activation(pages[n][:].indirect(places), p_sb[:], ACT.Copy)
-        nc.sync.dma_start(out[0:P, :], pages[0][:])
-        nc.scalar.dma_start(out[P : 2 * P, :], pages[1][:])
+                else:
+                    nc.vector.tensor_copy(p_sb[:], p_ps[:])
+                    nc.vector.tensor_copy(pages[n][:].indirect(places), p_sb[:])
+        nc.scalar.dma_start(out[0:P, :], pages[0][:])
+        nc.sync.dma_start(out[P : 2 * P, :], pages[1][:])

from contextlib import ExitStack

import concourse.mybir as mybir

K, T, J, R, N, E = 512, 1024, 256, 512, 256, 1024
FLOPS = 2 * (2 * K * R * J + R * N * J)

F32 = mybir.dt.float32
BF16 = mybir.dt.bfloat16
I32 = mybir.dt.int32
U32 = mybir.dt.uint32
U16 = mybir.dt.uint16
U8 = mybir.dt.uint8
E4M3 = mybir.dt.float8_e4m3fn_x4
E5M2 = mybir.dt.float8_e5m2_x4
E2M1 = mybir.dt.float4_e2m1fn_x4
ACT = mybir.ActivationFunctionType
ALU = mybir.AluOpType

P = 128
PACK = 4
HALF = J // 2


def tile_list_tablepartner_oneforboth_store_scattered_kernel(
    tc, xt_words, xt_scales, xo_words, xo_scales, w_words, w_scales, tg, sg, bg, vs_words, vs_scales,
    offs, offs2, offs3, offs4, offs5, offs6, out,
):
    nc = tc.nc
    with ExitStack() as ctx:
        lists = ctx.enter_context(tc.tile_pool(name="lists", bufs=1))
        keep = ctx.enter_context(tc.tile_pool(name="keep", bufs=1))
        psum = ctx.enter_context(tc.psum_pool(name="psum", bufs=1))

        def load_list(src, name):
            tile = lists.tile([P, J // 16], U16, name=name)
            nc.sync.dma_start(tile[:], src)
            return tile

        def scale_tile(engine, width, name):
            tile = keep.tile([P, width], U8, name=name, align_bytes=64)
            engine.memset(tile[:].bitcast(I32), 0)
            return tile

        def load_scales(queue, tile, src, quadrants):
            for q in quadrants:
                queue.dma_start(tile[32 * q : 32 * q + 4, :].bitcast(I32), src[0, 4 * q : 4 * q + 4, :].bitcast(I32))

        xo_sc = scale_tile(nc.vector, T, "xo_sc")
        xt_sc = scale_tile(nc.vector, T, "xt_sc")
        w_sc = scale_tile(nc.vector, R, "w_sc")
        vs_sc = scale_tile(nc.vector, T, "vs_sc")

        w_raw = keep.tile([P, R], U16, name="w_raw", align_bytes=64)
        xo_w = keep.tile([P, T], U32, name="xo_w", align_bytes=64)
        xt_w = keep.tile([P, T], U32, name="xt_w", align_bytes=64)
        vs_w = keep.tile([P, T], U16, name="vs_w", align_bytes=64)
        tg_rows = [keep.tile([P, T], F32, name=f"tg{t}") for t in range(PACK)]
        tg_view = tg.rearrange("(p t) q -> p t q", t=PACK)
        slope = keep.tile([P, PACK], F32, name="slope")
        shift = keep.tile([P, PACK], F32, name="shift")

        nc.sync.dma_start(w_raw[:].bitcast(I32), w_words[0].bitcast(I32))
        l_xo = load_list(offs2, "l_xo")
        load_scales(nc.sync, xo_sc, xo_scales, [0])
        load_scales(nc.sync, xo_sc, xo_scales, [1])
        load_scales(nc.sync, xo_sc, xo_scales, [2])
        load_scales(nc.sync, xo_sc, xo_scales, [3])
        load_scales(nc.sync, w_sc, w_scales, [0])
        nc.sync.dma_start(xo_w[:].bitcast(I32), xo_words[0].rearrange("p c t -> p (c t)").bitcast(I32))
        load_scales(nc.sync, w_sc, w_scales, [1])
        load_scales(nc.sync, w_sc, w_scales, [2])
        load_scales(nc.sync, w_sc, w_scales, [3])
        l_xt = load_list(offs, "l_xt")
        nc.sync.dma_start(xt_w[:].bitcast(I32), xt_words[0].rearrange("p c t -> p (c t)").bitcast(I32))
        load_scales(nc.sync, xt_sc, xt_scales, [0])
        load_scales(nc.sync, xt_sc, xt_scales, [1])
        nc.sync.dma_start(tg_rows[0][:], tg_view[:, 0, :])
        l_b = load_list(offs3, "l_b")
        l_tg = load_list(offs4, "l_tg")
        nc.sync.dma_start(slope[:], sg.rearrange("(p t) o -> p (t o)", t=PACK))
        nc.sync.dma_start(tg_rows[1][:], tg_view[:, 1, :])
        nc.sync.dma_start(shift[:], bg.rearrange("(p t) o -> p (t o)", t=PACK))
        nc.sync.dma_start(tg_rows[2][:], tg_view[:, 2, :])
        l_vs = load_list(offs5, "l_vs")
        load_scales(nc.sync, vs_sc, vs_scales, [0])
        load_scales(nc.sync, vs_sc, vs_scales, [1])
        nc.sync.dma_start(tg_rows[3][:], tg_view[:, 3, :])
        l_out = load_list(offs6, "l_out")
        nc.sync.dma_start(vs_w[:].bitcast(I32), vs_words[0].bitcast(I32))
        load_scales(nc.gpsimd, xt_sc, xt_scales, [2])
        load_scales(nc.gpsimd, xt_sc, xt_scales, [3])
        load_scales(nc.gpsimd, vs_sc, vs_scales, [2])
        load_scales(nc.gpsimd, vs_sc, vs_scales, [3])

        warm = keep.tile([P, 2], F32, name="warm")
        nc.vector.memset(warm[:, 0:1], 0.0)
        nc.scalar.activation(warm[:, 1:2], warm[:, 0:1], ACT.Sigmoid)
        pages = [keep.tile([P, E], F32, name=f"page{n}") for n in range(N // P)]
        for page in pages:
            nc.vector.memset(page[:], 0.0)

        w_cols = keep.tile([P, PACK, P], U16, name="w_cols", align_bytes=64)
        w_col_sc = keep.tile([P, PACK, P], U8, name="w_col_sc", align_bytes=64)
        nc.vector.tensor_copy(w_cols[:], w_raw[:].rearrange("p (m t) -> p t m", t=PACK))
        w_sc_view = w_sc[:].rearrange("p (m t) -> p t m", t=PACK)
        nc.vector.tensor_copy(w_col_sc[:, 0, :], w_sc_view[:, 0, :])
        nc.vector.tensor_copy(w_col_sc[:, 1:PACK, :], w_sc_view[:, 1:PACK, :])

        def gather(words, scales, offsets, name):
            got = keep.tile([P, J], words.dtype, name=name + "_w", align_bytes=64)
            got_sc = keep.tile([P, J], U8, name=name + "_sc", align_bytes=64)
            nc.vector.tensor_copy(got[:], words[:].indirect(offsets[:]))
            nc.vector.tensor_copy(got_sc[:], scales[:].indirect(offsets[:]))
            return got, got_sc

        xo_g, xo_g_sc = gather(xo_w, xo_sc, l_xo, "xo_g")
        b_ps = [psum.tile([P, J], F32, name=f"b_ps{t}", tag=f"bank{t}") for t in range(PACK)]
        for t in range(PACK):
            nc.tensor.matmul_mx(b_ps[t][:], lhsT=w_cols[:, t, :].bitcast(E2M1), lhsT_scale=w_col_sc[:, t, :],
                                rhs=xo_g[:].bitcast(E4M3), rhs_scale=xo_g_sc[:], start=True, stop=True)
        xt_g, xt_g_sc = gather(xt_w, xt_sc, l_xt, "xt_g")
        a_ps = [psum.tile([P, 2, J], F32, name=f"a_ps{u}") for u in range(2)]
        for t in range(PACK):
            nc.tensor.matmul_mx(a_ps[t // 2][:, t % 2, :], lhsT=w_cols[:, t, :].bitcast(E2M1), lhsT_scale=w_col_sc[:, t, :],
                                rhs=xt_g[:].bitcast(E5M2), rhs_scale=xt_g_sc[:], start=True, stop=True)

        b_sb = [keep.tile([P, 2 * J], F32, name=f"b_sb{t}") for t in range(PACK)]
        for t in range(PACK):
            nc.scalar.copy(b_sb[t][:, 0:J], b_ps[t][:])
        partner = [keep.tile([P, 2, J], F32, name=f"partner{u}") for u in range(2)]
        for t in range(PACK):
            picked = partner[t // 2][:, t % 2, :]
            if t < 2:
                nc.vector.tensor_copy(picked, b_sb[t][:].indirect(l_b[:]))
            else:
                nc.scalar.activation(picked, b_sb[t][:].indirect(l_b[:]), ACT.Copy)
        diff = keep.tile([P, PACK, J], F32, name="diff")
        for u in range(2):
            nc.vector.tensor_tensor(diff[:, 2 * u : 2 * u + 2, :], a_ps[u][:], partner[u][:], ALU.subtract)

        gate = keep.tile([P, PACK, J], F32, name="gate")
        for t in range(PACK):
            nc.scalar.activation(gate[:, t, :], tg_rows[t][:].indirect(l_tg[:]), ACT.Sigmoid,
                                 bias=shift[:, t : t + 1], scale=slope[:, t : t + 1])

        gated = keep.tile([P, PACK, J], F32, name="gated")
        nc.vector.tensor_tensor(gated[:, 0:2, :], diff[:, 0:2, :], gate[:, 0:2, :], ALU.mult)

        vs_g, vs_g_sc = gather(vs_w, vs_sc, l_vs, "vs_g")

        hid = [keep.tile([P, HALF * PACK], BF16, name=f"hid{h}", align_bytes=64) for h in range(2)]
        hid_q = [keep.tile([P, HALF], U32, name=f"hid_q{h}", align_bytes=64) for h in range(2)]
        hid_sc = [keep.tile([P, HALF], U8, name=f"hid_sc{h}", align_bytes=64) for h in range(2)]
        for h in range(2):
            cols = slice(h * HALF, (h + 1) * HALF)
            nc.vector.tensor_tensor(gated[:, 2:4, cols], diff[:, 2:4, cols], gate[:, 2:4, cols], ALU.mult)
            nc.scalar.activation(
                hid[h][:].rearrange("p (c i t) -> p c t i", i=4, t=PACK),
                gated[:, :, cols].rearrange("p t (c i) -> p c t i", i=4),
                ACT.Abs,
            )
        for h in range(2):
            nc.vector.quantize_mx(hid_q[h][:].bitcast(E4M3), hid_sc[h][:], hid[h][:])
        for h in range(2):
            places = l_out[:, h * HALF // 16 : (h + 1) * HALF // 16]
            for n in range(N // P):
                rows = slice(n * P, (n + 1) * P)
                p_ps = psum.tile([P, HALF], F32, name=f"p_ps{h}{n}", tag=f"bank{2 * h + n}")
                nc.tensor.matmul_mx(p_ps[:], lhsT=vs_g[:, rows].bitcast(E2M1), lhsT_scale=vs_g_sc[:, rows],
                                    rhs=hid_q[h][:].bitcast(E4M3), rhs_scale=hid_sc[h][:], start=True, stop=True)
                p_sb = keep.tile([P, HALF], F32, name=f"p_sb{h}{n}")
                if n == 0:
                    nc.scalar.copy(p_sb[:], p_ps[:])
                    nc.scalar.activation(pages[n][:].indirect(places), p_sb[:], ACT.Copy)
                else:
                    nc.vector.tensor_copy(p_sb[:], p_ps[:])
                    nc.vector.tensor_copy(pages[n][:].indirect(places), p_sb[:])
        nc.scalar.dma_start(out[0:P, :], pages[0][:])
        nc.sync.dma_start(out[P : 2 * P, :], pages[1][:])
